import numpy as np
import ml_dtypes

BF16 = ml_dtypes.bfloat16


def bf(x):
    return np.asarray(x, np.float32).astype(BF16)


def f32(x):
    return np.asarray(x, np.float32)


def f64(x):
    return np.asarray(x).astype(np.float64)


def striped(idx):
    return np.tile(idx.reshape(-1, 16).T, (8, 1))


S, A, K, M, N, E, Q = 512, 512, 128, 128, 384, 4, 96


def setup_inputs():
    return {"x": bf(np.random.standard_normal((A, S))), "wd": bf(np.random.standard_normal((A, M)) / np.sqrt(A)), "y": bf(np.random.standard_normal((K, N))), "w": bf(np.random.standard_normal((E, K, M)) / np.sqrt(K)), "offs": striped(np.random.permutation(S)[:N])}


def reference(x, wd, y, w, offs):
    idx = offs[:16].T.reshape(-1)
    z = f64(wd).T @ f64(x)
    for e in range(E):
        z[:, idx[e * Q : (e + 1) * Q]] += f64(w)[e].T @ f64(y)[:, e * Q : (e + 1) * Q]
    return z

@@ -1,0 +1,56 @@
+import concourse.mybir as mybir
+
+BF16, F32, U16 = mybir.dt.bfloat16, mybir.dt.float32, mybir.dt.uint16
+
+P = 128
+S = 512
+D = 512
+A = D // P
+N = 384
+E = 4
+Q = N // E
+OFFSETS_PER_COLUMN = 16
+HALVES = 2
+
+FLOPS = 2 * D * P * S + 2 * P * P * N
+
+
+def tile_rows_fillproj_none_kernel(tc, x, wd, y, w, offs, out):
+    nc = tc.nc
+    with (
+        tc.tile_pool(name="held", bufs=1) as held,
+        tc.psum_pool(name="psum", bufs=1) as psum,
+    ):
+        dense_weights = held.tile([P, A, P], BF16, name="dense_weights")
+        tokens = [held.tile([P, A // HALVES, S], BF16, name=f"tokens{h}") for h in range(HALVES)]
+        offsets = held.tile([P, N // OFFSETS_PER_COLUMN], U16, name="offsets")
+        expert_weights = held.tile([P, E, P], BF16, name="expert_weights")
+        packed = held.tile([P, N], BF16, name="packed")
+        result = held.tile([P, S], F32, name="result")
+        window = psum.tile([P, S], F32, name="window")
+
+        x_view = x.rearrange("(p a) s -> p a s", a=A)
+        nc.sync.dma_start(dense_weights[:], wd.rearrange("(p a) m -> p a m", a=A))
+        for h in range(HALVES):
+            nc.sync.dma_start(tokens[h][:], x_view[:, h * (A // HALVES) : (h + 1) * (A // HALVES), :])
+        nc.sync.dma_start(offsets[:], offs)
+        nc.sync.dma_start(expert_weights[:], w.rearrange("e k m -> k e m"))
+        nc.sync.dma_start(packed[:], y)
+
+        for a in range(A):
+            h, b = divmod(a, A // HALVES)
+            nc.tensor.matmul(window[:], dense_weights[:, a, :], tokens[h][:, b, :], start=(a == 0), stop=False)
+
+        per_expert = Q // OFFSETS_PER_COLUMN
+        for e in range(E):
+            piece = offsets[:, e * per_expert : (e + 1) * per_expert]
+            nc.tensor.matmul(
+                window[:].indirect(piece),
+                expert_weights[:, e, :],
+                packed[:, e * Q : (e + 1) * Q],
+                start=False,
+                stop=(e == E - 1),
+            )
+
+        nc.vector.tensor_copy(result[:], window[:])
+        nc.sync.dma_start(out, result[:])

@@ -10,6 +10,7 @@ N = 384
 E = 4
 Q = N // E
 OFFSETS_PER_COLUMN = 16
+WARM_UP = 5
 HALVES = 2
 
 FLOPS = 2 * D * P * S + 2 * P * P * N
@@ -28,6 +29,12 @@ def tile_rows_fillproj_none_kernel(tc, x, wd, y, w, offs, out):
         packed = held.tile([P, N], BF16, name="packed")
         result = held.tile([P, S], F32, name="result")
         window = psum.tile([P, S], F32, name="window")
+
+        zeros = held.tile([P, S], BF16, name="zeros")
+        spare_bank = psum.tile([P, S], F32, name="spare_bank")
+        nc.vector.memset(zeros[:], 0.0)
+        for i in range(WARM_UP):
+            nc.tensor.matmul(spare_bank[:], zeros[:, :P], zeros[:], start=True, stop=True)
 
         x_view = x.rearrange("(p a) s -> p a s", a=A)
         nc.sync.dma_start(dense_weights[:], wd.rearrange("(p a) m -> p a m", a=A))

@@ -10,7 +10,7 @@ N = 384
 E = 4
 Q = N // E
 OFFSETS_PER_COLUMN = 16
-WARM_UP = 5
+WARM_UP = 3
 HALVES = 2
 
 FLOPS = 2 * D * P * S + 2 * P * P * N
@@ -59,5 +59,7 @@ def tile_rows_fillproj_none_kernel(tc, x, wd, y, w, offs, out):
                 stop=(e == E - 1),
             )
 
-        nc.vector.tensor_copy(result[:], window[:])
-        nc.sync.dma_start(out, result[:])
+        for h in range(HALVES):
+            half = slice(h * (S // HALVES), (h + 1) * (S // HALVES))
+            nc.vector.tensor_copy(result[:, half], window[:, half])
+            nc.sync.dma_start(out[:, half], result[:, half])

import concourse.mybir as mybir

BF16, F32, U16 = mybir.dt.bfloat16, mybir.dt.float32, mybir.dt.uint16

P = 128
S = 512
D = 512
A = D // P
N = 384
E = 4
Q = N // E
OFFSETS_PER_COLUMN = 16
WARM_UP = 3
HALVES = 2

FLOPS = 2 * D * P * S + 2 * P * P * N


def tile_rows_fillproj_none_kernel(tc, x, wd, y, w, offs, out):
    nc = tc.nc
    with (
        tc.tile_pool(name="held", bufs=1) as held,
        tc.psum_pool(name="psum", bufs=1) as psum,
    ):
        dense_weights = held.tile([P, A, P], BF16, name="dense_weights")
        tokens = [held.tile([P, A // HALVES, S], BF16, name=f"tokens{h}") for h in range(HALVES)]
        offsets = held.tile([P, N // OFFSETS_PER_COLUMN], U16, name="offsets")
        expert_weights = held.tile([P, E, P], BF16, name="expert_weights")
        packed = held.tile([P, N], BF16, name="packed")
        result = held.tile([P, S], F32, name="result")
        window = psum.tile([P, S], F32, name="window")

        zeros = held.tile([P, S], BF16, name="zeros")
        spare_bank = psum.tile([P, S], F32, name="spare_bank")
        nc.vector.memset(zeros[:], 0.0)
        for i in range(WARM_UP):
            nc.tensor.matmul(spare_bank[:], zeros[:, :P], zeros[:], start=True, stop=True)

        x_view = x.rearrange("(p a) s -> p a s", a=A)
        nc.sync.dma_start(dense_weights[:], wd.rearrange("(p a) m -> p a m", a=A))
        for h in range(HALVES):
            nc.sync.dma_start(tokens[h][:], x_view[:, h * (A // HALVES) : (h + 1) * (A // HALVES), :])
        nc.sync.dma_start(offsets[:], offs)
        nc.sync.dma_start(expert_weights[:], w.rearrange("e k m -> k e m"))
        nc.sync.dma_start(packed[:], y)

        for a in range(A):
            h, b = divmod(a, A // HALVES)
            nc.tensor.matmul(window[:], dense_weights[:, a, :], tokens[h][:, b, :], start=(a == 0), stop=False)

        per_expert = Q // OFFSETS_PER_COLUMN
        for e in range(E):
            piece = offsets[:, e * per_expert : (e + 1) * per_expert]
            nc.tensor.matmul(
                window[:].indirect(piece),
                expert_weights[:, e, :],
                packed[:, e * Q : (e + 1) * Q],
                start=False,
                stop=(e == E - 1),
            )

        for h in range(HALVES):
            half = slice(h * (S // HALVES), (h + 1) * (S // HALVES))
            nc.vector.tensor_copy(result[:, half], window[:, half])
            nc.sync.dma_start(out[:, half], result[:, half])
